import numpy as np, ml_dtypes
CORES = [35,38,43,46]
N = 4
import mx_ref
BF = ml_dtypes.bfloat16
def f(rng, *shape):
    return mx_ref.flush((rng.standard_normal(shape, dtype=np.float32) * np.exp2(rng.integers(-2, 3, shape[:-1] + (1,)))).astype(BF))
def wide(rng, *shape, cols=0):
    v = rng.standard_normal(shape, dtype=np.float32) * np.exp2(rng.integers(-12, 13, shape)).astype(np.float32)
    if cols: v *= np.repeat(np.exp2(rng.integers(-cols, cols + 1, shape[:-2] + (1, shape[-1] // 4))) * (rng.random(shape[:-2] + (1, shape[-1] // 4)) > 0.0625), 4, axis=-1).astype(np.float32)
    return mx_ref.flush(v.astype(BF))
T, NB, CH, BW = 512, 4, 128, 128
def scores(x, u):
    return np.stack([mx_ref.matmul(mx_ref.quantize(u[s]), mx_ref.quantize(x[s]))[0] for s in range(N)]) + np.float32(0.0)
def dealt(rng, d, place):
    v = d["x"].reshape(N, 128, T, 4).transpose(0, 2, 1, 3).reshape(N * T, 128, 4)
    g = np.argsort(-scores(d["x"], d["u"]).reshape(-1), kind="stable")
    e = np.stack([g[rng.permutation(place[s])] for s in range(N)])
    return np.ascontiguousarray(v[e].transpose(0, 2, 1, 3)).reshape(N, 128, 4 * T)
def setup_inputs(rng):
    u = np.zeros((N, 128, 512), BF); u[:, :, :4] = f(rng, 128, 4)
    return {"x": f(rng, N, 128, 4 * T), "u": u, "w": f(rng, N, 128, 512 * NB)}
def setup_inputs_ties(rng):
    d = setup_inputs(rng); d["u"][:, 64:] = 0; few = f(rng, 64, 24).reshape(64, 6, 4)
    for s in range(N):
        e = rng.permutation(np.concatenate([np.arange(6), rng.choice(6, T - 6, p=rng.dirichlet(np.ones(6)))]))
        d["x"][s, :64] = few[:, e].reshape(64, -1)
    return d
def setup_inputs_blocks(rng):
    d = setup_inputs(rng); d["x"] = dealt(rng, d, np.arange(N * T).reshape(N, T)[rng.permutation(N)]); return d
def setup_inputs_alternate(rng):
    d = setup_inputs(rng); d["x"] = dealt(rng, d, np.arange(N * T).reshape(T, N).T[rng.permutation(N)]); return d
def setup_inputs_zeros(rng):
    d = setup_inputs(rng); d["u"][:, 64:] = 0
    for s in rng.permutation(N)[:N // 2]: d["x"][s, :64] = 0
    return d
def setup_inputs_spread(rng):
    d = setup_inputs(rng); k = np.where(rng.permutation(N) < N // 2, np.float32(2.0 ** -20), np.float32(2.0 ** 7))
    d["x"] = mx_ref.flush((wide(rng, N, 128, 4 * T, cols=8).astype(np.float32) * k[:, None, None]).astype(BF))
    d["u"] = (d["u"].astype(np.float32) * np.float32(2 ** 24)).astype(BF); return d
def check_inputs(d):
    b = []; u = np.asarray(d["u"]).astype(np.float32)
    for r in range(N):
        if (u[r][:, 4:] != 0).any() or (u[r] != u[0]).any(): b.append("u")
    return b
def reference(x, u, w):
    score = scores(x, u)
    order = [np.argsort(-score[s], kind="stable") for s in range(N)]
    y = np.zeros((N, 128, T), np.float32); ids = np.zeros((N, 2, T), np.float32)
    for d in range(N):
        runs = [order[s][CH * d:CH * d + CH] for s in range(N)]
        rank = np.repeat(np.arange(N), CH); col = np.concatenate(runs)
        m = np.argsort(-score[rank, col], kind="stable")
        rank, col = rank[m], col[m]
        ids[d, 0], ids[d, 1] = rank, col
        t = np.ascontiguousarray(x.reshape(N, 128, T, 4)[rank, :, col].transpose(1, 0, 2)).reshape(128, 4 * T)
        for k in range(NB):
            W = mx_ref.quantize(np.ascontiguousarray(w[d][:, 512 * k:512 * k + 512]))
            y[d][:, BW * k:BW * k + BW] = mx_ref.matmul(W, mx_ref.quantize(np.ascontiguousarray(t[:, 4 * BW * k:4 * BW * k + 4 * BW])))
    return {"y": y, "ids": ids}

@@ -1,0 +1,309 @@
+from concourse.bass import DstId, RemoteDMATransfer
+from concourse.mybir import dt, AluOpType as A, ActivationFunctionType as F
+
+N, CH = 4, 128
+X4 = "float8_e4m3fn_x4"
+
+
+def _sb(n, d):
+    return ("sbuf", [128, n], d)
+
+
+SCRATCH = {
+    "xt": _sb(2048, "bfloat16"), "wt": _sb(2048, "bfloat16"), "ut": _sb(512, "bfloat16"),
+    "xq": _sb(512, X4), "xs": _sb(512, "uint8"), "wq": _sb(512, X4), "ws": _sb(512, "uint8"),
+    "uq": _sb(128, X4), "us": _sb(128, "uint8"), "ubq": _sb(128, X4), "ubs": _sb(128, "uint8"),
+    "sq": _sb(384, X4), "sp": _sb(384, "uint8"), "lq": _sb(512, X4), "lp": _sb(512, "uint8"),
+    "fq": _sb(512, X4), "fp": _sb(512, "uint8"),
+    "zoff": _sb(8, "uint16"), "half": _sb(128, "bfloat16"), "tri": _sb(128, "bfloat16"), "ip": _sb(2, "int32"),
+    "it": _sb(32, "int32"), "it2": _sb(32, "int32"), "pl": _sb(32, "uint16"), "r3": _sb(2, "int32"),
+    "rep1": _sb(2, "uint16"), "rep2": _sb(2, "uint16"), "p15": _sb(2, "int32"), "corr0": _sb(2, "float32"),
+    "corr": _sb(2, "float32"), "pcol": _sb(2, "float32"), "ibias": _sb(2, "float32"), "bl32": _sb(8, "int32"),
+    "bl": _sb(8, "uint16"), "de": _sb(128, "int32"), "de2": _sb(128, "int32"), "da": _sb(128, "float32"),
+    "db": _sb(128, "float32"), "d0": _sb(512, "float32"), "idv": _sb(512, "bfloat16"),
+    "ss": _sb(512, "float32"), "vc": _sb(4, "float32"), "sg": _sb(512, "bfloat16"), "cb": _sb(2048, "bfloat16"),
+    "es": _sb(768, "bfloat16"), "fsn": _sb(256, "bfloat16"), "pr": _sb(32, "bfloat16"), "pt": _sb(32, "bfloat16"),
+    "pu": _sb(32, "uint16"), "pw": _sb(32, "uint16"), "sl": _sb(512, "float32"), "so": _sb(512, "float32"),
+    "tr": _sb(512, "float32"), "v16": _sb(16, "float32"), "wi": _sb(512, "bfloat16"), "wx": _sb(512, "float32"),
+    "lw": _sb(32, "uint16"), "tw": _sb(512, "bfloat16"), "twc": _sb(16, "float32"),
+    "rs": _sb(32, "float32"), "ri": _sb(16, "float32"), "bx": _sb(512, "float32"), "sb": _sb(512, "float32"),
+    "v1": _sb(4, "float32"), "sg2": _sb(768, "bfloat16"), "c2": _sb(1536, "bfloat16"), "f2": _sb(768, "bfloat16"),
+    "pr2": _sb(32, "bfloat16"), "pt2": _sb(32, "bfloat16"), "pu2": _sb(32, "uint16"), "pw2": _sb(32, "uint16"),
+    "wi2": _sb(512, "bfloat16"), "wx2": _sb(512, "float32"), "lm": _sb(32, "uint16"),
+    "inn": _sb(512, "bfloat16"), "iw": _sb(512, "bfloat16"), "gid": _sb(512, "float32"), "ysb": _sb(512, "float32"),
+    "ps": ("psum", [128, 4096], "float32"),
+}
+SEMAPHORES = ["v", "a", "t", "q", "du", "dx0", "dx1", "dx2", "dx3", "dw", "dp1", "dp2", "dst",
+              "rem_s", "rem_c", "rem_p", "rem_i", "loc"]
+
+
+def _routes(core, cores, topo):
+    far = [c for c in cores if c != core and topo.chip(c) != topo.chip(core)]
+    near = [c for c in cores if c != core and topo.chip(c) == topo.chip(core)]
+    out, used = {}, set()
+    for i, c in enumerate(far):
+        e = topo.engines(core, c)
+        k = 1
+        while 2 * k * len(far) <= len(e):
+            k *= 2
+        out[c] = e[i * k:i * k + k]
+        used.update(out[c])
+    for i, c in enumerate(near):
+        e = [n for n in topo.engines(core, c) if n not in used]
+        k = 1
+        while 2 * k * len(near) <= len(e):
+            k *= 2
+        out[c] = e[i * k:i * k + k]
+    return out
+
+
+def rank_program(g, core, T, topo):
+    rank = T.rank_of(core)
+    if rank is None:
+        return
+    cores = T.cores
+    others = [d for d in range(N) if d != rank]
+    routes = _routes(core, cores, topo)
+    arrive = sum(len(_routes(c, cores, topo)[core]) for c in cores if c != core)
+    U32, U8 = dt.uint32, dt.uint8
+
+    V = {"q": g.vector, "sem": "v", "n": 0, "seen": {}}
+    S = {"q": g.scalar, "sem": "a", "n": 0, "seen": {}}
+    P = {"q": g.tensor, "sem": "t", "n": 0, "seen": {}}
+    G = {"q": g, "sem": "q", "n": 0, "seen": {}}
+    Y = {"q": g.sync, "sem": None, "n": 0, "seen": {}}
+    dmas = {}
+
+    def need(E, deps):
+        for s, n in deps:
+            if E["seen"].get(s, 0) < n:
+                E["q"].wait_ge(T.sem[s], n)
+                E["seen"][s] = n
+
+    def op(E, deps, call, *a, **k):
+        need(E, deps)
+        call(*a, **k).then_inc(T.sem[E["sem"]], 1)
+        E["n"] += 1
+        return (E["sem"], E["n"])
+
+    def dma(E, deps, out, in_, sem):
+        need(E, deps)
+        E["q"].dma_start(out, in_).then_inc(T.sem[sem], 16)
+        dmas[sem] = dmas.get(sem, 0) + 16
+        return (sem, dmas[sem])
+
+    def send(deps, pieces, sem):
+        need(G, deps)
+        tr = []
+        for d, src, dst in pieces:
+            rid, pid, _ = topo.addr(cores[d])
+            tr.append(RemoteDMATransfer(dst_ids=[DstId(rid=rid, pnc=pid)],
+                                        dma_engine_mask=sum(1 << e for e in routes[cores[d]]),
+                                        remote_sem=T.sem[sem], src=src, dst=dst))
+            dmas["loc"] = dmas.get("loc", 0) + len(routes[cores[d]])
+        g.remote_dma_fused(tr, local_sem=T.sem.loc)
+
+    vec, act, pe = g.vector, g.scalar.activation, g.tensor.matmul_mx
+    cp, ts, tt, scan = vec.tensor_copy, vec.tensor_scalar, vec.tensor_tensor, vec.tensor_tensor_scan
+
+    du = dma(Y, [], T.ut[:, 0:8], T.u[:, 0:8], "du")
+    dx = [None] * 4
+    for c in range(4):
+        dx[c] = dma(S if c & 1 else Y, [], T.xt[:, 512 * c:512 * c + 512], T.x[:, 512 * c:512 * c + 512], "dx%d" % c)
+    dw = dma(Y, [], T.wt[:], T.w[:], "dw")
+
+    m0 = op(V, [], vec.memset, T.ut[:, 8:512], 0.0)
+    mz = op(V, [], vec.memset, T.zoff[:], 0)
+    mh = op(V, [], vec.memset, T.half[:], 0.5)
+    k_ip = op(G, [], g.iota, T.ip[:], [[0, 2]], 0, 1)
+    k_it = op(G, [], g.iota, T.it[:], [[1, 32]], 0, 32)
+    k_de = op(G, [], g.iota, T.de[:], [[1, 128]], 2048, -1)
+    k_bl = op(G, [], g.iota, T.bl32[:], [[1, 4], [0, 2]], 0, 0)
+    k_pc = op(G, [], g.iota, T.pcol[:], [[0, 2]], -256, 1, allow_small_or_imprecise_dtypes=True)
+    k_tri = op(G, [mh], g.affine_select, T.tri[:], T.half[:], [[-1, 128]], A.is_gt, -0.5, 0, 1)
+    k_id = op(G, [], g.iota, T.idv[:], [[1, 32], [32, 16]], -256, 0, allow_small_or_imprecise_dtypes=True)
+    a3 = op(V, [k_ip], ts, T.r3[:], T.ip[:], 3, None, A.bitwise_and)
+    a15 = op(V, [k_ip], ts, T.p15[:], T.ip[:], 15, None, A.bitwise_and)
+    apl = op(V, [k_it], ts, T.it2[:], T.it[:], 511, None, A.bitwise_and)
+    ade = op(V, [k_de], ts, T.de2[:], T.de[:], 15, None, A.bitwise_and)
+    k_r1 = op(V, [a3], ts, T.rep1[:], T.r3[:], 64, 63, A.mult, A.add)
+    k_r2 = op(V, [a3], ts, T.rep2[:], T.r3[:], 192, 191, A.mult, A.add)
+    k_c0 = op(V, [a15], ts, T.corr0[:], T.p15[:], 15, 1024, A.is_lt, A.mult)
+    k_pl = op(V, [apl], cp, T.pl[:], T.it2[:])
+    k_da = op(V, [ade], ts, T.da[:], T.de2[:], 0, -4096, A.is_equal, A.mult)
+    k_db = op(V, [ade], ts, T.db[:], T.de2[:], 1, 1024, A.is_equal, A.mult)
+    k_co = op(V, [k_c0], ts, T.corr[:], T.corr0[:], 256, None, A.subtract)
+    k_bl = op(V, [k_bl], cp, T.bl[:], T.bl32[:])
+    k_ib = op(V, [k_pc], ts, T.ibias[:], T.pcol[:], -255, 256, A.is_equal, A.mult)
+    k_d0 = op(V, [k_da, k_db], tt, T.d0[:, 0:128], T.da[:], T.db[:], A.add)
+
+    qu = op(V, [m0, du], vec.quantize_mx, T.uq[:], T.us[:], T.ut[:])
+    ub = op(V, [qu, mz], cp, T.ubq[:, 0:128].bitcast(U32), T.uq[:, 0:128].bitcast(U32).indirect(T.zoff[:, 0:8]))
+    ubs = op(S, [qu, mz], act, T.ubs[:, 0:128], T.us[:, 0:128].indirect(T.zoff[:, 0:8]), F.Copy)
+    kd = k_d0
+    for i in range(1, 4):
+        kd = op(S, [k_d0], act, T.d0[:, 128 * i:128 * i + 128], T.d0[:, 0:128], F.Copy)
+
+    def r(c, w=128):
+        return slice(w * c, w * c + w)
+
+    qx, pv, psc, vcol, sc, sgn = [None] * 4, [None] * 4, [None] * 4, [None] * 4, [None] * 4, [None] * 4
+
+    def quant(c):
+        qx[c] = op(V, [dx[c]], vec.quantize_mx, T.xq[:, r(c)], T.xs[:, r(c)], T.xt[:, r(c, 512)])
+        b = 512 * (4 + c)
+        pv[c] = op(P, [qx[c], ub, ubs], pe, T.ps[:, b:b + 128], T.xq[:, r(c)], T.xs[:, r(c)], T.ubq[:], T.ubs[:], True, True)
+        b = 512 * c
+        psc[c] = op(P, [], pe, T.ps[:, b:b + 128], T.ubq[:], T.ubs[:], T.xq[:, r(c)], T.xs[:, r(c)], True, True)
+
+    def cb(c, a, b):
+        return T.cb[:, 512 * c + a:512 * c + b]
+
+    def work_a(c):
+        vcol[c] = op(V, [pv[c]], cp, T.vc[:, c:c + 1], T.ps[:, 512 * (4 + c):512 * (4 + c) + 1])
+        sc[c] = op(S, [psc[c]], act, T.ss[:, r(c)], T.ps[:, 512 * c:512 * c + 128], F.Copy)
+        sgn[c] = op(S, [vcol[c]], act, T.sg[:, r(c)], T.ps[:, 512 * c:512 * c + 128], F.Sign, T.vc[:, c:c + 1], -1.0)
+        if c:
+            return op(V, [vcol[c], sc[c - 1]], ts, cb(c, 0, 128 * c), T.ss[:, 0:128 * c], T.vc[:, c:c + 1], None, A.is_ge)
+
+    def work_b(c, e):
+        return op(V, [sc[c]], ts, cb(e, 128 * c, 128 * c + 128), T.ss[:, r(c)], T.vc[:, e:e + 1], None, A.is_gt)
+
+    def work_d(c):
+        return op(V, [sgn[c], k_tri], tt, cb(c, 128 * c, 128 * c + 128), T.sg[:, r(c)], T.tri[:], A.is_lt)
+
+    def early(c, dep):
+        return op(V, [dep], scan, T.es[:, r(c, 192)], cb(c, 0, 192), cb(c, 192, 384), -256.0, A.add, A.add)
+
+    def late(c, dep):
+        return op(V, dep, scan, T.fsn[:, r(c, 64)], cb(c, 384, 448), cb(c, 448, 512),
+                  T.es[:, 192 * c + 191:192 * c + 192], A.add, A.add)
+
+    quant(0)
+    quant(1)
+    work_a(0)
+    work_d(0)
+    quant(2)
+    work_a(1)
+    work_b(1, 0)
+    work_d(1)
+    work_a(2)
+    quant(3)
+    b0 = work_b(2, 0)
+    b1 = work_b(2, 1)
+    b2 = work_d(2)
+    e0 = early(0, b0)
+    e1 = early(1, b1)
+    e2 = early(2, b2)
+    w3 = work_a(3)
+    b0 = work_b(3, 0)
+    e3 = early(3, w3)
+    b1 = work_b(3, 1)
+    b2 = work_b(3, 2)
+    b3 = work_d(3)
+    late(0, [b0, e0])
+    late(1, [b1, e1])
+    late(2, [b2, e2])
+    fin = late(3, [b3, e3])
+    sl = op(S, [k_pl, sc[3]], act, T.sl[:, 0:512], T.ss[:, 0:512].indirect(T.pl[:, 0:32]), F.Copy)
+
+    def wrap(fin, src, rep, pr, pt, pu, pw, sem):
+        x = op(V, [fin], cp, pr[:, 0:32], src.indirect(rep[:, 0:2]))
+        x = op(V, [x], vec.transpose, pt[:], pr[:])
+        x = op(V, [x], ts, pu[:], pt[:], 256, None, A.add)
+        for a in range(4):
+            z = dma(Y if a < 2 else S, [x], pw[a:128:4, 0:32], pu[32 * a:32 * a + 32, 0:32], sem)
+        return z
+
+    dp1 = wrap(fin, T.fsn[:, 0:256], T.rep1, T.pr, T.pt, T.pu, T.pw, "dp1")
+
+    qw = op(V, [dw], vec.quantize_mx, T.wq[:], T.ws[:], T.wt[:])
+    mi = op(V, [], vec.memset, T.inn[:], 0.0)
+    for s in range(1, N):
+        mi2 = op(V, [mi], vec.memset, T.inn[:, 128 * s:128 * s + 128:32], float(s))
+
+    x = op(V, [dp1, sl], cp, T.so[:, 0:512].indirect(T.pw[:, 0:32]), T.sl[:, 0:512])
+    so = x
+    x = op(V, [x], vec.transpose, T.tr[:], T.so[:])
+    v16 = op(V, [x], cp, T.v16[:], T.tr[:, 0:512:32])
+    send([v16], [(d, T.v16[:, 4 * d:4 * d + 4], T.rs[:, 8 * rank:8 * rank + 4]) for d in others], "rem_s")
+    sbo = op(S, [so], act, T.sb[:, r(rank)], T.so[:, r(rank)], F.Copy)
+    rso = op(S, [v16], act, T.rs[:, 8 * rank:8 * rank + 4], T.v16[:, 4 * rank:4 * rank + 4], F.Copy)
+
+    wi = op(V, [dp1, k_id], cp, T.wi[:, 0:512].indirect(T.pw[:, 0:32]), T.idv[:, 0:512])
+
+    def lists(dep, w, wx, out):
+        x = op(V, [dep, kd], scan, wx[:], T.d0[:], w[:], 0.0, A.add, A.max)
+        return op(V, [x, k_co], ts, out[:, 0:32], wx[:, 15:512:16], T.corr[:, 0:1], None, A.subtract)
+
+    lw = lists(wi, T.wi, T.wx, T.lw)
+    for i, d in enumerate(others):
+        of = T.lw[:, 8 * d:8 * d + 8]
+        pq = op(V, [lw], cp, T.sq[:, r(i)].bitcast(U32), T.xq[:, 0:512].bitcast(U32).indirect(of))
+        pp = op(S, [lw], act, T.sp[:, r(i)], T.xs[:, 0:512].indirect(of), F.Copy)
+    send([pq], [(d, T.sq[:, r(i)].bitcast(U8), T.lq[:, r(rank)].bitcast(U8)) for i, d in enumerate(others)], "rem_c")
+    send([pp], [(d, T.sp[:, r(i)], T.lp[:, r(rank)]) for i, d in enumerate(others)], "rem_p")
+
+    rem_s = ("rem_s", arrive)
+    for a in range(4):
+        q = slice(32 * a, 32 * a + 32)
+        v1 = op(S, [rem_s, rso], act, T.v1[q, 0:4], T.rs[q, a:32:8], F.Copy)
+    for d in others:
+        x = op(V, [rem_s], cp, T.bx[:, r(d)], T.rs[:, 8 * d:8 * d + 4].indirect(T.bl[:, 0:8]))
+        tb = op(V, [x], vec.transpose, T.sb[:, r(d)], T.bx[:, r(d)])
+
+    def seg(s):
+        return [(0, 128 * s, 0, True)] * (s > 0) + [(128 * s + 128, 512, 128 * s, False)] * (s < 3)
+
+    sg2 = {}
+    for s in (2, 3):
+        for lo, hi, at, ge in seg(s):
+            o = 384 * (s - 2) + at
+            sg2[s] = op(S, [v1, tb, sbo], act, T.sg2[:, o:o + hi - lo], T.sb[:, lo:hi], F.Sign, T.v1[:, s:s + 1], -1.0)
+    for s in range(N):
+        for lo, hi, at, ge in seg(s):
+            out = T.c2[:, 384 * s + at:384 * s + at + hi - lo]
+            if s < 2:
+                x = op(V, [v1, tb, sbo], ts, out, T.sb[:, lo:hi], T.v1[:, s:s + 1], None, A.is_ge if ge else A.is_gt)
+            else:
+                o = 384 * (s - 2) + at
+                x = op(V, [sg2[s]], ts, out, T.sg2[:, o:o + hi - lo], 0.0, None, A.is_le if ge else A.is_lt)
+        fin2 = op(V, [x, k_pc], scan, T.f2[:, r(s, 192)], T.c2[:, 384 * s:384 * s + 192],
+                  T.c2[:, 384 * s + 192:384 * s + 384], T.pcol[:, 0:1], A.add, A.add)
+    dp2 = wrap(fin2, T.f2[:, 0:768], T.rep2, T.pr2, T.pt2, T.pu2, T.pw2, "dp2")
+
+    of = T.lw[:, 8 * rank:8 * rank + 8]
+    x = op(V, [wi], vec.transpose, T.tw[:], T.wi[:])
+    tw = op(V, [x], cp, T.twc[:], T.tw[:, 0:512:32])
+    oq = op(V, [lw], cp, T.lq[:, r(rank)].bitcast(U32), T.xq[:, 0:512].bitcast(U32).indirect(of))
+    ow = op(S, [lw], act, T.lp[:, r(rank)], T.xs[:, 0:512].indirect(of), F.Copy)
+    send([tw], [(d, T.twc[:, 4 * d:4 * d + 4], T.ri[:, 4 * rank:4 * rank + 4]) for d in others], "rem_i")
+    rio = op(S, [tw], act, T.ri[:, 4 * rank:4 * rank + 4], T.twc[:, 4 * rank:4 * rank + 4], F.Copy)
+
+    wi2 = op(V, [dp2], cp, T.wi2[:, 0:512].indirect(T.pw2[:, 0:32]), T.idv[:, 0:512])
+    lm = lists(wi2, T.wi2, T.wx2, T.lm)
+    ym, yc = [None] * 4, [None] * 4
+
+    def ycopy(k):
+        if k == 3:
+            yc[k] = op(V, [ym[k]], cp, T.ysb[:, r(k)], T.ps[:, 512 * k:512 * k + 128])
+        else:
+            yc[k] = op(S, [ym[k]], act, T.ysb[:, r(k)], T.ps[:, 512 * k:512 * k + 128], F.Copy)
+        dma(Y, [yc[k]], T.y[:, r(k)], T.ysb[:, r(k)], "dst")
+
+    for k in range(4):
+        of = T.lm[:, 8 * k:8 * k + 8]
+        a = op(V, [lm, oq, ("rem_c", arrive)], cp, T.fq[:, r(k)].bitcast(U32), T.lq[:, 0:512].bitcast(U32).indirect(of))
+        b = op(S, [lm, ow, ("rem_p", arrive)], act, T.fp[:, r(k)], T.lp[:, 0:512].indirect(of), F.Copy)
+        ym[k] = op(P, [a, b, qw], pe, T.ps[:, 512 * k:512 * k + 128], T.wq[:, r(k)], T.ws[:, r(k)], T.fq[:, r(k)], T.fp[:, r(k)], True, True)
+        if k:
+            ycopy(k - 1)
+    ic = op(S, [rio, mi2, ("rem_i", arrive)], act, T.inn[:, 1:512:32], T.ri[:], F.Copy)
+    iw = op(V, [ic, mi2], vec.transpose, T.iw[:], T.inn[:])
+    i1 = op(S, [iw, k_ib], act, T.gid[:, 256:512], T.iw[:, 0:512].indirect(T.lm[:, 16:32]), F.Identity, T.ibias[:, 0:1])
+    ycopy(3)
+    i0 = op(V, [iw, k_ib], ts, T.gid[:, 0:256], T.iw[:, 0:512].indirect(T.lm[:, 0:16]), T.ibias[:, 0:1], None, A.add)
+    dma(Y, [i0, i1], T.ids[:], T.gid[0:2, 0:512], "dst")
+
+    need(Y, [("dst", dmas["dst"])])
+    need(G, [("loc", dmas["loc"]), ("v", V["n"]), ("a", S["n"]), ("t", P["n"]), ("q", G["n"])])

@@ -16,24 +16,31 @@ SCRATCH = {
     "sq": _sb(384, X4), "sp": _sb(384, "uint8"), "lq": _sb(512, X4), "lp": _sb(512, "uint8"),
     "fq": _sb(512, X4), "fp": _sb(512, "uint8"),
     "zoff": _sb(8, "uint16"), "half": _sb(128, "bfloat16"), "tri": _sb(128, "bfloat16"), "ip": _sb(2, "int32"),
-    "it": _sb(32, "int32"), "it2": _sb(32, "int32"), "pl": _sb(32, "uint16"), "r3": _sb(2, "int32"),
-    "rep1": _sb(2, "uint16"), "rep2": _sb(2, "uint16"), "p15": _sb(2, "int32"), "corr0": _sb(2, "float32"),
-    "corr": _sb(2, "float32"), "pcol": _sb(2, "float32"), "ibias": _sb(2, "float32"), "bl32": _sb(8, "int32"),
-    "bl": _sb(8, "uint16"), "de": _sb(128, "int32"), "de2": _sb(128, "int32"), "da": _sb(128, "float32"),
-    "db": _sb(128, "float32"), "d0": _sb(512, "float32"), "idv": _sb(512, "bfloat16"),
-    "ss": _sb(512, "float32"), "vc": _sb(4, "float32"), "sg": _sb(512, "bfloat16"), "cb": _sb(2048, "bfloat16"),
-    "es": _sb(768, "bfloat16"), "fsn": _sb(256, "bfloat16"), "pr": _sb(32, "bfloat16"), "pt": _sb(32, "bfloat16"),
-    "pu": _sb(32, "uint16"), "pw": _sb(32, "uint16"), "sl": _sb(512, "float32"), "so": _sb(512, "float32"),
-    "tr": _sb(512, "float32"), "v16": _sb(16, "float32"), "wi": _sb(512, "bfloat16"), "wx": _sb(512, "float32"),
-    "lw": _sb(32, "uint16"), "tw": _sb(512, "bfloat16"), "twc": _sb(16, "float32"),
-    "rs": _sb(32, "float32"), "ri": _sb(16, "float32"), "bx": _sb(512, "float32"), "sb": _sb(512, "float32"),
-    "v1": _sb(4, "float32"), "sg2": _sb(768, "bfloat16"), "c2": _sb(1536, "bfloat16"), "f2": _sb(768, "bfloat16"),
-    "pr2": _sb(32, "bfloat16"), "pt2": _sb(32, "bfloat16"), "pu2": _sb(32, "uint16"), "pw2": _sb(32, "uint16"),
-    "wi2": _sb(512, "bfloat16"), "wx2": _sb(512, "float32"), "lm": _sb(32, "uint16"),
-    "inn": _sb(512, "bfloat16"), "iw": _sb(512, "bfloat16"), "gid": _sb(512, "float32"), "ysb": _sb(512, "float32"),
+    "r3": _sb(2, "int32"), "p15": _sb(2, "int32"), "p12": _sb(2, "int32"), "p96": _sb(2, "int32"),
+    "p16": _sb(2, "int32"), "p31": _sb(2, "int32"), "corr0": _sb(2, "float32"), "corr": _sb(2, "float32"),
+    "corw0": _sb(2, "float32"), "corw": _sb(2, "float32"), "quad": _sb(2, "float32"), "tok0": _sb(2, "float32"),
+    "tok": _sb(2, "float32"), "k4": _sb(8, "int32"), "plq": _sb(8, "uint16"), "lo": _sb(2, "float32"),
+    "hi": _sb(2, "float32"), "pcol": _sb(2, "float32"), "ibias": _sb(2, "float32"), "bl32": _sb(32, "int32"),
+    "bl": _sb(32, "uint16"),
+    "de": _sb(16, "int32"), "de2": _sb(16, "int32"), "da": _sb(16, "bfloat16"), "db": _sb(16, "bfloat16"),
+    "d0": _sb(512, "bfloat16"), "dg": _sb(32, "int32"), "dg2": _sb(32, "int32"), "dga": _sb(32, "bfloat16"),
+    "dgb": _sb(32, "bfloat16"), "d4": _sb(32, "bfloat16"), "zz": _sb(136, "bfloat16"),
+    "idv0": _sb(128, "bfloat16"), "idv": _sb(128, "bfloat16"),
+    "ss": _sb(512, "float32"), "vc": _sb(4, "float32"), "sg": _sb(512, "bfloat16"), "sgb": _sb(768, "bfloat16"),
+    "cb": _sb(2080, "bfloat16"), "es": _sb(768, "bfloat16"), "z1": _sb(544, "bfloat16"),
+    "sl": _sb(128, "float32"), "so": _sb(512, "float32"), "tr": _sb(512, "float32"), "v16": _sb(16, "float32"),
+    "rs": _sb(16, "float32"), "r1": _sb(16, "float32"), "rr": _sb(16, "float32"), "bx": _sb(512, "float32"),
+    "sb": _sb(512, "float32"), "v1": _sb(4, "float32"), "sg2": _sb(768, "bfloat16"), "c2": _sb(1600, "bfloat16"),
+    "z2": _sb(800, "bfloat16"), "li": _sb(32, "uint16"), "ia": _sb(16, "bfloat16"), "ib": _sb(16, "bfloat16"),
+    "inn": _sb(512, "bfloat16"), "iw": _sb(512, "bfloat16"), "q2": _sb(8, "uint16"), "gid": _sb(128, "float32"),
+    "ysb": _sb(512, "float32"),
     "ps": ("psum", [128, 4096], "float32"),
 }
-SEMAPHORES = ["v", "a", "t", "q", "du", "dx0", "dx1", "dx2", "dx3", "dw", "dp1", "dp2", "dst",
+for _k in ("1", "2"):
+    SCRATCH.update({"pt" + _k: _sb(32, "bfloat16"), "pg" + _k: _sb(32, "float16"), "pw" + _k: _sb(8, "uint16"),
+                    "wi" + _k: _sb(512, "bfloat16"), "wx" + _k: _sb(512, "float16"), "ge" + _k: _sb(32, "float16"),
+                    "gm" + _k: _sb(32, "float16"), "lw" + _k: _sb(32, "uint16")})
+SEMAPHORES = ["v", "a", "t", "q", "du", "dx0", "dx1", "dx2", "dx3", "dw", "dst",
               "rem_s", "rem_c", "rem_p", "rem_i", "loc"]
 
 
@@ -64,7 +71,12 @@ def rank_program(g, core, T, topo):
     cores = T.cores
     others = [d for d in range(N) if d != rank]
     routes = _routes(core, cores, topo)
-    arrive = sum(len(_routes(c, cores, topo)[core]) for c in cores if c != core)
+    FEW = 4
+
+    def arrive(sem):
+        n = [len(_routes(c, cores, topo)[core]) for c in cores if c != core]
+        return (sem, sum(min(k, FEW) for k in n) if sem == "rem_s" else sum(n))
+
     U32, U8 = dt.uint32, dt.uint8
 
     V = {"q": g.vector, "sem": "v", "n": 0, "seen": {}}
@@ -97,77 +109,93 @@ def rank_program(g, core, T, topo):
         tr = []
         for d, src, dst in pieces:
             rid, pid, _ = topo.addr(cores[d])
+            engines = routes[cores[d]][:FEW] if sem == "rem_s" else routes[cores[d]]
             tr.append(RemoteDMATransfer(dst_ids=[DstId(rid=rid, pnc=pid)],
-                                        dma_engine_mask=sum(1 << e for e in routes[cores[d]]),
+                                        dma_engine_mask=sum(1 << e for e in engines),
                                         remote_sem=T.sem[sem], src=src, dst=dst))
-            dmas["loc"] = dmas.get("loc", 0) + len(routes[cores[d]])
+            dmas["loc"] = dmas.get("loc", 0) + len(engines)
         g.remote_dma_fused(tr, local_sem=T.sem.loc)
 
     vec, act, pe = g.vector, g.scalar.activation, g.tensor.matmul_mx
     cp, ts, tt, scan = vec.tensor_copy, vec.tensor_scalar, vec.tensor_tensor, vec.tensor_tensor_scan
 
-    du = dma(Y, [], T.ut[:, 0:8], T.u[:, 0:8], "du")
+    def r(c, w=128):
+        return slice(w * c, w * c + w)
+
+    def iota(out, pattern, base, mult, small=True):
+        return op(G, [], g.iota, out, pattern, base, mult, allow_small_or_imprecise_dtypes=small)
+
     dx = [None] * 4
-    for c in range(4):
-        dx[c] = dma(S if c & 1 else Y, [], T.xt[:, 512 * c:512 * c + 512], T.x[:, 512 * c:512 * c + 512], "dx%d" % c)
+    dx[0] = dma(Y, [], T.xt[:, r(0, 512)], T.x[:, r(0, 512)], "dx0")
+    du = dma(S, [], T.ut[:, 0:8], T.u[:, 0:8], "du")
+    for c in (1, 2, 3):
+        dx[c] = dma(S if c & 1 else Y, [], T.xt[:, r(c, 512)], T.x[:, r(c, 512)], "dx%d" % c)
     dw = dma(Y, [], T.wt[:], T.w[:], "dw")
 
+    k_ip = iota(T.ip[:], [[0, 2]], 0, 1, False)
+    k_de = iota(T.de[:], [[1, 16]], 2048, -1, False)
+    k_dg = iota(T.dg[:], [[4, 32]], 2051, -1, False)
+    k_k4 = iota(T.k4[:], [[4, 8]], 0, 0, False)
+    mh = op(V, [], vec.memset, T.half[:], 0.5)
     m0 = op(V, [], vec.memset, T.ut[:, 8:512], 0.0)
     mz = op(V, [], vec.memset, T.zoff[:], 0)
-    mh = op(V, [], vec.memset, T.half[:], 0.5)
-    k_ip = op(G, [], g.iota, T.ip[:], [[0, 2]], 0, 1)
-    k_it = op(G, [], g.iota, T.it[:], [[1, 32]], 0, 32)
-    k_de = op(G, [], g.iota, T.de[:], [[1, 128]], 2048, -1)
-    k_bl = op(G, [], g.iota, T.bl32[:], [[1, 4], [0, 2]], 0, 0)
-    k_pc = op(G, [], g.iota, T.pcol[:], [[0, 2]], -256, 1, allow_small_or_imprecise_dtypes=True)
     k_tri = op(G, [mh], g.affine_select, T.tri[:], T.half[:], [[-1, 128]], A.is_gt, -0.5, 0, 1)
-    k_id = op(G, [], g.iota, T.idv[:], [[1, 32], [32, 16]], -256, 0, allow_small_or_imprecise_dtypes=True)
+    k_i0 = iota(T.idv0[:], [[4, 8], [1, 4], [128, 4]], -256, 0)
+    for c in range(4):
+        iota(T.cb[:, 520 * c + 512:520 * c + 520], [[0, 8]], 0, 0)
+    k_zz = iota(T.zz[:], [[0, 136]], 0, 0)
+    mw1 = iota(T.wi1[:], [[0, 512]], -512, 0)
+    k_bl = iota(T.bl32[:], [[1, 16], [0, 2]], 0, 0, False)
+    for s in range(N):
+        for b in (192, 392):
+            iota(T.c2[:, 400 * s + b:400 * s + b + 8], [[0, 8]], 0, 0)
+    k_pc = iota(T.pcol[:], [[0, 2]], -256, 1)
+    mi = iota(T.inn[:], [[1, 4], [0, 128]], 0, 0)
+    a96 = op(V, [k_ip], ts, T.p96[:], T.ip[:], 96, None, A.bitwise_and)
     a3 = op(V, [k_ip], ts, T.r3[:], T.ip[:], 3, None, A.bitwise_and)
     a15 = op(V, [k_ip], ts, T.p15[:], T.ip[:], 15, None, A.bitwise_and)
-    apl = op(V, [k_it], ts, T.it2[:], T.it[:], 511, None, A.bitwise_and)
+    a12 = op(V, [k_ip], ts, T.p12[:], T.ip[:], 12, None, A.bitwise_and)
+    k_qd = op(V, [a96], ts, T.quad[:], T.p96[:], 1, None, A.mult)
     ade = op(V, [k_de], ts, T.de2[:], T.de[:], 15, None, A.bitwise_and)
-    k_r1 = op(V, [a3], ts, T.rep1[:], T.r3[:], 64, 63, A.mult, A.add)
-    k_r2 = op(V, [a3], ts, T.rep2[:], T.r3[:], 192, 191, A.mult, A.add)
+    adg = op(V, [k_dg], ts, T.dg2[:], T.dg[:], 12, None, A.bitwise_and)
     k_c0 = op(V, [a15], ts, T.corr0[:], T.p15[:], 15, 1024, A.is_lt, A.mult)
-    k_pl = op(V, [apl], cp, T.pl[:], T.it2[:])
-    k_da = op(V, [ade], ts, T.da[:], T.de2[:], 0, -4096, A.is_equal, A.mult)
-    k_db = op(V, [ade], ts, T.db[:], T.de2[:], 1, 1024, A.is_equal, A.mult)
-    k_co = op(V, [k_c0], ts, T.corr[:], T.corr0[:], 256, None, A.subtract)
-    k_bl = op(V, [k_bl], cp, T.bl[:], T.bl32[:])
-    k_ib = op(V, [k_pc], ts, T.ibias[:], T.pcol[:], -255, 256, A.is_equal, A.mult)
-    k_d0 = op(V, [k_da, k_db], tt, T.d0[:, 0:128], T.da[:], T.db[:], A.add)
+    k_w0 = op(V, [a12], ts, T.corw0[:], T.p12[:], 12, 1024, A.is_lt, A.mult)
+    for i in range(4):
+        ms = op(S, [mh], act, T.so[:, r(i)], T.half[:], F.Copy, 0.0, -1e29)
+    k_id = op(S, [k_i0, k_qd], act, T.idv[:], T.idv0[:], F.Identity, T.quad[:, 0:1])
 
     qu = op(V, [m0, du], vec.quantize_mx, T.uq[:], T.us[:], T.ut[:])
     ub = op(V, [qu, mz], cp, T.ubq[:, 0:128].bitcast(U32), T.uq[:, 0:128].bitcast(U32).indirect(T.zoff[:, 0:8]))
     ubs = op(S, [qu, mz], act, T.ubs[:, 0:128], T.us[:, 0:128].indirect(T.zoff[:, 0:8]), F.Copy)
-    kd = k_d0
-    for i in range(1, 4):
-        kd = op(S, [k_d0], act, T.d0[:, 128 * i:128 * i + 128], T.d0[:, 0:128], F.Copy)
-
-    def r(c, w=128):
-        return slice(w * c, w * c + w)
 
     qx, pv, psc, vcol, sc, sgn = [None] * 4, [None] * 4, [None] * 4, [None] * 4, [None] * 4, [None] * 4
+    sgb = {}
 
     def quant(c):
         qx[c] = op(V, [dx[c]], vec.quantize_mx, T.xq[:, r(c)], T.xs[:, r(c)], T.xt[:, r(c, 512)])
         b = 512 * (4 + c)
-        pv[c] = op(P, [qx[c], ub, ubs], pe, T.ps[:, b:b + 128], T.xq[:, r(c)], T.xs[:, r(c)], T.ubq[:], T.ubs[:], True, True)
+        pv[c] = op(P, [qx[c], qu], pe, T.ps[:, b:b + 128], T.xq[:, r(c)], T.xs[:, r(c)], T.uq[:], T.us[:], True, True)
         b = 512 * c
-        psc[c] = op(P, [], pe, T.ps[:, b:b + 128], T.ubq[:], T.ubs[:], T.xq[:, r(c)], T.xs[:, r(c)], True, True)
+        psc[c] = op(P, [ub, ubs], pe, T.ps[:, b:b + 128], T.ubq[:], T.ubs[:], T.xq[:, r(c)], T.xs[:, r(c)], True, True)
 
     def cb(c, a, b):
-        return T.cb[:, 512 * c + a:512 * c + b]
+        return T.cb[:, 520 * c + a:520 * c + b]
+
+    def at_b(c, e):
+        return r(c * (c - 1) // 2 + e)
 
     def work_a(c):
+        row = T.ps[:, 512 * c:512 * c + 128]
         vcol[c] = op(V, [pv[c]], cp, T.vc[:, c:c + 1], T.ps[:, 512 * (4 + c):512 * (4 + c) + 1])
-        sc[c] = op(S, [psc[c]], act, T.ss[:, r(c)], T.ps[:, 512 * c:512 * c + 128], F.Copy)
-        sgn[c] = op(S, [vcol[c]], act, T.sg[:, r(c)], T.ps[:, 512 * c:512 * c + 128], F.Sign, T.vc[:, c:c + 1], -1.0)
+        for e in range(c):
+            sgb[c, e] = op(S, [psc[c], vcol[e]], act, T.sgb[:, at_b(c, e)], row, F.Sign, T.vc[:, e:e + 1], -1.0)
+        sgn[c] = op(S, [psc[c], vcol[c]], act, T.sg[:, r(c)], row, F.Sign, T.vc[:, c:c + 1], -1.0)
+        sc[c] = op(S, [], act, T.ss[:, r(c)], row, F.Copy)
         if c:
             return op(V, [vcol[c], sc[c - 1]], ts, cb(c, 0, 128 * c), T.ss[:, 0:128 * c], T.vc[:, c:c + 1], None, A.is_ge)
 
     def work_b(c, e):
-        return op(V, [sc[c]], ts, cb(e, 128 * c, 128 * c + 128), T.ss[:, r(c)], T.vc[:, e:e + 1], None, A.is_gt)
+        return op(V, [sgb[c, e]], ts, cb(e, 128 * c, 128 * c + 128), T.sgb[:, at_b(c, e)], 0.0, None, A.is_lt)
 
     def work_d(c):
         return op(V, [sgn[c], k_tri], tt, cb(c, 128 * c, 128 * c + 128), T.sg[:, r(c)], T.tri[:], A.is_lt)
@@ -176,13 +204,24 @@ def rank_program(g, core, T, topo):
         return op(V, [dep], scan, T.es[:, r(c, 192)], cb(c, 0, 192), cb(c, 192, 384), -256.0, A.add, A.add)
 
     def late(c, dep):
-        return op(V, dep, scan, T.fsn[:, r(c, 64)], cb(c, 384, 448), cb(c, 448, 512),
+        return op(V, dep + [k_zz], scan, T.z1[:, c:544:4], cb(c, 384, 520), T.zz[:, 0:136],
                   T.es[:, 192 * c + 191:192 * c + 192], A.add, A.add)
 
     quant(0)
     quant(1)
+    k_ga = op(V, [adg], ts, T.dga[:], T.dg2[:], 0, -4096, A.is_equal, A.mult)
+    k_gb = op(V, [adg], ts, T.dgb[:], T.dg2[:], 4, 1024, A.is_equal, A.mult)
+    k_da = op(V, [ade], ts, T.da[:], T.de2[:], 0, -4096, A.is_equal, A.mult)
+    k_db = op(V, [ade], ts, T.db[:], T.de2[:], 1, 1024, A.is_equal, A.mult)
+    k_t0 = op(V, [k_qd], ts, T.tok0[:], T.r3[:], 128, T.quad[:, 0:1], A.mult, A.add)
     work_a(0)
+    k_d4 = op(V, [k_ga, k_gb], tt, T.d4[:], T.dga[:], T.dgb[:], A.add)
+    k_d0 = op(V, [k_da, k_db], tt, T.d0[:, 0:16], T.da[:], T.db[:], A.add)
+    k_co = op(V, [k_c0], ts, T.corr[:], T.corr0[:], 256, None, A.subtract)
+    k_cw = op(V, [k_w0], ts, T.corw[:], T.corw0[:], 256, None, A.subtract)
+    k_tk = op(V, [k_t0], ts, T.tok[:], T.p12[:], 0.25, T.tok0[:, 0:1], A.mult, A.add)
     work_d(0)
+    k_pl = op(V, [k_tk, k_k4], ts, T.plq[:], T.k4[:], T.tok[:, 0:1], None, A.add)
     quant(2)
     work_a(1)
     work_b(1, 0)
@@ -197,60 +236,95 @@ def rank_program(g, core, T, topo):
     e2 = early(2, b2)
     w3 = work_a(3)
     b0 = work_b(3, 0)
-    e3 = early(3, w3)
     b1 = work_b(3, 1)
     b2 = work_b(3, 2)
+    e3 = early(3, w3)
     b3 = work_d(3)
     late(0, [b0, e0])
     late(1, [b1, e1])
     late(2, [b2, e2])
     fin = late(3, [b3, e3])
-    sl = op(S, [k_pl, sc[3]], act, T.sl[:, 0:512], T.ss[:, 0:512].indirect(T.pl[:, 0:32]), F.Copy)
+    sl = op(S, [k_pl, sc[3]], act, T.sl[:, 0:128], T.ss[:, 0:512].indirect(T.plq[:, 0:8]), F.Copy)
+    kd = k_d0
+    for n in (16, 32, 64, 128, 256):
+        kd = op(S, [kd], act, T.d0[:, n:2 * n], T.d0[:, 0:n], F.Copy)
+    for i in range(4):
+        mw2 = op(S, [mh], act, T.wi2[:, r(i)], T.half[:], F.Copy, 0.0, -1024.0)
 
-    def wrap(fin, src, rep, pr, pt, pu, pw, sem):
-        x = op(V, [fin], cp, pr[:, 0:32], src.indirect(rep[:, 0:2]))
-        x = op(V, [x], vec.transpose, pt[:], pr[:])
-        x = op(V, [x], ts, pu[:], pt[:], 256, None, A.add)
+    def offsets(fin, z, k, fill=None):
+        x = op(V, [fin], vec.transpose, T["pt" + k][:], z)
+        if fill:
+            fill()
+        x = op(V, [x, k_d4], scan, T["pg" + k][:], T.d4[:], T["pt" + k][:], 0.0, A.add, A.max)
+        return op(V, [x, k_cw], ts, T["pw" + k][:, 0:8], T["pg" + k][:, 3:32:4], T.corw[:, 0:1], None, A.subtract)
+
+    def scatter(x, k, mw):
+        return op(V, [x, k_id, mw], cp, T["wi" + k][:, 0:512].indirect(T["pw" + k][:, 0:8]), T.idv[:, 0:128])
+
+    def diagonal(x, k):
+        return op(V, [x, kd], scan, T["wx" + k][:], T.d0[:], T["wi" + k][:], 0.0, A.add, A.max)
+
+    def quadrants(x, mid, out, w, src):
         for a in range(4):
-            z = dma(Y if a < 2 else S, [x], pw[a:128:4, 0:32], pu[32 * a:32 * a + 32, 0:32], sem)
+            p, o = slice(32 * a, 32 * a + 32), slice(32 * (a ^ 1), 32 * (a ^ 1) + 32)
+            y = op(V, x, tt, mid[p, 0:w], src(p), src(o), A.max)
+        for a in range(2):
+            p, o = slice(64 * a, 64 * a + 64), slice(64 * (a ^ 1), 64 * (a ^ 1) + 64)
+            z = op(V, [y], tt, out[p, 0:w], mid[p, 0:w], mid[o, 0:w], A.max)
         return z
 
-    dp1 = wrap(fin, T.fsn[:, 0:256], T.rep1, T.pr, T.pt, T.pu, T.pw, "dp1")
+    def number_list(x, k):
+        wx = T["wx" + k]
+        x = quadrants([x], T["ge" + k], T["gm" + k], 32, lambda p: wx[p, 15:512:16])
+        return x, op(V, [x, k_co], ts, T["lw" + k][:, 0:32], T["gm" + k][:, 0:32], T.corr[:, 0:1], None, A.subtract)
 
-    qw = op(V, [dw], vec.quantize_mx, T.wq[:], T.ws[:], T.wt[:])
-    mi = op(V, [], vec.memset, T.inn[:], 0.0)
-    for s in range(1, N):
-        mi2 = op(V, [mi], vec.memset, T.inn[:, 128 * s:128 * s + 128:32], float(s))
-
-    x = op(V, [dp1, sl], cp, T.so[:, 0:512].indirect(T.pw[:, 0:32]), T.sl[:, 0:512])
-    so = x
-    x = op(V, [x], vec.transpose, T.tr[:], T.so[:])
+    pw = offsets(fin, T.z1[:, 512:544], "1")
+    so = op(V, [pw, sl, ms], cp, T.so[:, 0:512].indirect(T.pw1[:, 0:8]), T.sl[:, 0:128])
+    wi = scatter(pw, "1", mw1)
+    x = op(V, [so], vec.transpose, T.tr[:], T.so[:])
+    wx = diagonal(wi, "1")
     v16 = op(V, [x], cp, T.v16[:], T.tr[:, 0:512:32])
-    send([v16], [(d, T.v16[:, 4 * d:4 * d + 4], T.rs[:, 8 * rank:8 * rank + 4]) for d in others], "rem_s")
-    sbo = op(S, [so], act, T.sb[:, r(rank)], T.so[:, r(rank)], F.Copy)
-    rso = op(S, [v16], act, T.rs[:, 8 * rank:8 * rank + 4], T.v16[:, 4 * rank:4 * rank + 4], F.Copy)
+    send([v16], [(d, T.v16[:, 4 * d:4 * d + 4], T.rs[:, 4 * rank:4 * rank + 4]) for d in others], "rem_s")
+    rso = op(S, [v16], act, T.rs[:, 4 * rank:4 * rank + 4], T.v16[:, 4 * rank:4 * rank + 4], F.Copy)
+    gm, lw = number_list(wx, "1")
+    send([lw], [(d, T.lw1[:, 8 * d:8 * d + 8], T.li[:, 8 * rank:8 * rank + 8]) for d in others], "rem_i")
 
-    wi = op(V, [dp1, k_id], cp, T.wi[:, 0:512].indirect(T.pw[:, 0:32]), T.idv[:, 0:512])
-
-    def lists(dep, w, wx, out):
-        x = op(V, [dep, kd], scan, wx[:], T.d0[:], w[:], 0.0, A.add, A.max)
-        return op(V, [x, k_co], ts, out[:, 0:32], wx[:, 15:512:16], T.corr[:, 0:1], None, A.subtract)
-
-    lw = lists(wi, T.wi, T.wx, T.lw)
+    spans = []
     for i, d in enumerate(others):
-        of = T.lw[:, 8 * d:8 * d + 8]
-        pq = op(V, [lw], cp, T.sq[:, r(i)].bitcast(U32), T.xq[:, 0:512].bitcast(U32).indirect(of))
-        pp = op(S, [lw], act, T.sp[:, r(i)], T.xs[:, 0:512].indirect(of), F.Copy)
+        if spans and spans[-1][1] + spans[-1][2] == d:
+            spans[-1][2] += 1
+        else:
+            spans.append([i, d, 1])
+    for i, d, n in spans:
+        of = T.lw1[:, 8 * d:8 * d + 8 * n]
+        at = slice(128 * i, 128 * i + 128 * n)
+        pq = op(V, [lw], cp, T.sq[:, at].bitcast(U32), T.xq[:, 0:512].bitcast(U32).indirect(of))
+        pp = op(S, [lw], act, T.sp[:, at], T.xs[:, 0:512].indirect(of), F.Copy)
     send([pq], [(d, T.sq[:, r(i)].bitcast(U8), T.lq[:, r(rank)].bitcast(U8)) for i, d in enumerate(others)], "rem_c")
     send([pp], [(d, T.sp[:, r(i)], T.lp[:, r(rank)]) for i, d in enumerate(others)], "rem_p")
 
-    rem_s = ("rem_s", arrive)
+    of = T.lw1[:, 8 * rank:8 * rank + 8]
+    sbo = op(V, [lw], cp, T.sb[:, r(rank)], T.ss[:, 0:512].indirect(of))
+    k_bl = op(V, [k_bl], cp, T.bl[:], T.bl32[:])
+    oq = op(V, [lw], cp, T.lq[:, r(rank)].bitcast(U32), T.xq[:, 0:512].bitcast(U32).indirect(of))
+    ow = op(S, [lw], act, T.lp[:, r(rank)], T.xs[:, 0:512].indirect(of), F.Copy)
+    lio = op(V, [lw], cp, T.li[:, 8 * rank:8 * rank + 8], of)
+    a16 = op(V, [k_ip], ts, T.p16[:], T.ip[:], 16, None, A.bitwise_and)
+    a31 = op(V, [k_ip], ts, T.p31[:], T.ip[:], 31, None, A.bitwise_and)
+    k_lo = op(V, [a16], ts, T.lo[:], T.p16[:], 16, None, A.is_lt)
+    k_hi = op(V, [a16], ts, T.hi[:], T.p16[:], 16, None, A.is_equal)
+    k_ib = op(V, [a31], ts, T.ibias[:], T.p31[:], 1, 256, A.is_equal, A.mult)
+    qw = op(V, [dw], vec.quantize_mx, T.wq[:], T.ws[:], T.wt[:])
+
+    rr = quadrants([arrive("rem_s"), rso], T.r1, T.rr, 16, lambda p: T.rs[p, 0:16])
+    sx = others[2]
+    bx = {sx: op(S, [rr, k_bl], act, T.bx[:, r(sx)], T.rr[:, 0:16].indirect(T.bl[:, 8 * sx:8 * sx + 8]), F.Copy)}
     for a in range(4):
-        q = slice(32 * a, 32 * a + 32)
-        v1 = op(S, [rem_s, rso], act, T.v1[q, 0:4], T.rs[q, a:32:8], F.Copy)
+        v1 = op(S, [rr], act, T.v1[32 * a:32 * a + 32, 0:4], T.rr[32 * a:32 * a + 32, a:16:4], F.Copy)
+    for d in others[:2]:
+        bx[d] = op(V, [rr, k_bl], cp, T.bx[:, r(d)], T.rr[:, 0:16].indirect(T.bl[:, 8 * d:8 * d + 8]))
     for d in others:
-        x = op(V, [rem_s], cp, T.bx[:, r(d)], T.rs[:, 8 * d:8 * d + 4].indirect(T.bl[:, 0:8]))
-        tb = op(V, [x], vec.transpose, T.sb[:, r(d)], T.bx[:, r(d)])
+        tb = op(V, [bx[d]], vec.transpose, T.sb[:, r(d)], T.bx[:, r(d)])
 
     def seg(s):
         return [(0, 128 * s, 0, True)] * (s > 0) + [(128 * s + 128, 512, 128 * s, False)] * (s < 3)
@@ -260,50 +334,59 @@ def rank_program(g, core, T, topo):
         for lo, hi, at, ge in seg(s):
             o = 384 * (s - 2) + at
             sg2[s] = op(S, [v1, tb, sbo], act, T.sg2[:, o:o + hi - lo], T.sb[:, lo:hi], F.Sign, T.v1[:, s:s + 1], -1.0)
+    done = []
     for s in range(N):
         for lo, hi, at, ge in seg(s):
-            out = T.c2[:, 384 * s + at:384 * s + at + hi - lo]
-            if s < 2:
-                x = op(V, [v1, tb, sbo], ts, out, T.sb[:, lo:hi], T.v1[:, s:s + 1], None, A.is_ge if ge else A.is_gt)
-            else:
-                o = 384 * (s - 2) + at
-                x = op(V, [sg2[s]], ts, out, T.sg2[:, o:o + hi - lo], 0.0, None, A.is_le if ge else A.is_lt)
-        fin2 = op(V, [x, k_pc], scan, T.f2[:, r(s, 192)], T.c2[:, 384 * s:384 * s + 192],
-                  T.c2[:, 384 * s + 192:384 * s + 384], T.pcol[:, 0:1], A.add, A.add)
-    dp2 = wrap(fin2, T.f2[:, 0:768], T.rep2, T.pr2, T.pt2, T.pu2, T.pw2, "dp2")
+            end = at + hi - lo
+            for b, e in ([(at, 192), (192, end)] if at < 192 < end else [(at, end)]):
+                w = 400 * s + b + 8 * (b >= 192)
+                out = T.c2[:, w:w + e - b]
+                if s < 2:
+                    x = op(V, [v1, tb, sbo], ts, out, T.sb[:, lo + b - at:lo + e - at], T.v1[:, s:s + 1], None,
+                           A.is_ge if ge else A.is_gt)
+                else:
+                    o = 384 * (s - 2)
+                    x = op(V, [sg2[s]], ts, out, T.sg2[:, o + b:o + e], 0.0, None, A.is_le if ge else A.is_lt)
+        done.append(x)
+    for s in range(N):
+        fin2 = op(V, [done[s], k_pc], scan, T.z2[:, s:800:4], T.c2[:, 400 * s:400 * s + 200],
+                  T.c2[:, 400 * s + 200:400 * s + 400], T.pcol[:, 0:1], A.add, A.add)
 
-    of = T.lw[:, 8 * rank:8 * rank + 8]
-    x = op(V, [wi], vec.transpose, T.tw[:], T.wi[:])
-    tw = op(V, [x], cp, T.twc[:], T.tw[:, 0:512:32])
-    oq = op(V, [lw], cp, T.lq[:, r(rank)].bitcast(U32), T.xq[:, 0:512].bitcast(U32).indirect(of))
-    ow = op(S, [lw], act, T.lp[:, r(rank)], T.xs[:, 0:512].indirect(of), F.Copy)
-    send([tw], [(d, T.twc[:, 4 * d:4 * d + 4], T.ri[:, 4 * rank:4 * rank + 4]) for d in others], "rem_i")
-    rio = op(S, [tw], act, T.ri[:, 4 * rank:4 * rank + 4], T.twc[:, 4 * rank:4 * rank + 4], F.Copy)
+    ids = []
 
-    wi2 = op(V, [dp2], cp, T.wi2[:, 0:512].indirect(T.pw2[:, 0:32]), T.idv[:, 0:512])
-    lm = lists(wi2, T.wi2, T.wx2, T.lm)
-    ym, yc = [None] * 4, [None] * 4
+    def halves():
+        ids.append(op(V, [lio, k_lo, arrive("rem_i")], ts, T.ia[:], T.li[:, 0:32:2], 256, T.lo[:, 0:1], A.subtract, A.mult))
+        ids.append(op(V, [k_hi], ts, T.ib[:], T.li[:, 1:32:2], 256, T.hi[:, 0:1], A.subtract, A.mult))
 
-    def ycopy(k):
-        if k == 3:
-            yc[k] = op(V, [ym[k]], cp, T.ysb[:, r(k)], T.ps[:, 512 * k:512 * k + 128])
-        else:
-            yc[k] = op(S, [ym[k]], act, T.ysb[:, r(k)], T.ps[:, 512 * k:512 * k + 128], F.Copy)
-        dma(Y, [yc[k]], T.y[:, r(k)], T.ysb[:, r(k)], "dst")
+    x = offsets(fin2, T.z2[:, 768:800], "2", halves)
+    ic = op(V, ids + [mi], tt, T.inn[:, 1:512:32], T.ia[:], T.ib[:], A.add)
+    x = scatter(x, "2", mw2)
+    x = diagonal(x, "2")
+    iw = op(V, [ic], vec.transpose, T.iw[:], T.inn[:])
+    gm, lm = number_list(x, "2")
 
+    def quad_list(a):
+        p = slice(32 * a, 32 * a + 32)
+        return op(V, [gm], ts, T.q2[p, 0:8], T.gm2[p, 8 * a:8 * a + 8], T.corr[p, 0:1], None, A.subtract)
+
+    quad_list(0)
+    quad_list(1)
+    ym = [None] * 4
     for k in range(4):
-        of = T.lm[:, 8 * k:8 * k + 8]
-        a = op(V, [lm, oq, ("rem_c", arrive)], cp, T.fq[:, r(k)].bitcast(U32), T.lq[:, 0:512].bitcast(U32).indirect(of))
-        b = op(S, [lm, ow, ("rem_p", arrive)], act, T.fp[:, r(k)], T.lp[:, 0:512].indirect(of), F.Copy)
+        of = T.lw2[:, 8 * k:8 * k + 8]
+        a = op(V, [lm, oq, arrive("rem_c")], cp, T.fq[:, r(k)].bitcast(U32), T.lq[:, 0:512].bitcast(U32).indirect(of))
+        b = op(S, [lm, ow, arrive("rem_p")], act, T.fp[:, r(k)], T.lp[:, 0:512].indirect(of), F.Copy)
         ym[k] = op(P, [a, b, qw], pe, T.ps[:, 512 * k:512 * k + 128], T.wq[:, r(k)], T.ws[:, r(k)], T.fq[:, r(k)], T.fp[:, r(k)], True, True)
-        if k:
-            ycopy(k - 1)
-    ic = op(S, [rio, mi2, ("rem_i", arrive)], act, T.inn[:, 1:512:32], T.ri[:], F.Copy)
-    iw = op(V, [ic, mi2], vec.transpose, T.iw[:], T.inn[:])
-    i1 = op(S, [iw, k_ib], act, T.gid[:, 256:512], T.iw[:, 0:512].indirect(T.lm[:, 16:32]), F.Identity, T.ibias[:, 0:1])
-    ycopy(3)
-    i0 = op(V, [iw, k_ib], ts, T.gid[:, 0:256], T.iw[:, 0:512].indirect(T.lm[:, 0:16]), T.ibias[:, 0:1], None, A.add)
-    dma(Y, [i0, i1], T.ids[:], T.gid[0:2, 0:512], "dst")
+    quad_list(2)
+    ql = quad_list(3)
+    for k in range(3):
+        yc = op(S, [ym[k]], act, T.ysb[:, r(k)], T.ps[:, 512 * k:512 * k + 128], F.Copy)
+        dma(Y, [yc], T.y[:, r(k)], T.ysb[:, r(k)], "dst")
+    ig = op(V, [ql, iw, k_ib], ts, T.gid[:, 0:128], T.iw[:, 0:512].indirect(T.q2[:, 0:8]), T.ibias[:, 0:1], None, A.add)
+    for a in range(4):
+        dma(Y, [ig], T.ids[:, r(a)], T.gid[32 * a:32 * a + 2, 0:128], "dst")
+    yc = op(V, [ym[3]], cp, T.ysb[:, r(3)], T.ps[:, 512 * 3:512 * 3 + 128])
+    dma(S, [yc], T.y[:, r(3)], T.ysb[:, r(3)], "dst")
 
     need(Y, [("dst", dmas["dst"])])
     need(G, [("loc", dmas["loc"]), ("v", V["n"]), ("a", S["n"]), ("t", P["n"]), ("q", G["n"])])

from concourse.bass import DstId, RemoteDMATransfer
from concourse.mybir import dt, AluOpType as A, ActivationFunctionType as F

N, CH = 4, 128
X4 = "float8_e4m3fn_x4"


def _sb(n, d):
    return ("sbuf", [128, n], d)


SCRATCH = {
    "xt": _sb(2048, "bfloat16"), "wt": _sb(2048, "bfloat16"), "ut": _sb(512, "bfloat16"),
    "xq": _sb(512, X4), "xs": _sb(512, "uint8"), "wq": _sb(512, X4), "ws": _sb(512, "uint8"),
    "uq": _sb(128, X4), "us": _sb(128, "uint8"), "ubq": _sb(128, X4), "ubs": _sb(128, "uint8"),
    "sq": _sb(384, X4), "sp": _sb(384, "uint8"), "lq": _sb(512, X4), "lp": _sb(512, "uint8"),
    "fq": _sb(512, X4), "fp": _sb(512, "uint8"),
    "zoff": _sb(8, "uint16"), "half": _sb(128, "bfloat16"), "tri": _sb(128, "bfloat16"), "ip": _sb(2, "int32"),
    "r3": _sb(2, "int32"), "p15": _sb(2, "int32"), "p12": _sb(2, "int32"), "p96": _sb(2, "int32"),
    "p16": _sb(2, "int32"), "p31": _sb(2, "int32"), "corr0": _sb(2, "float32"), "corr": _sb(2, "float32"),
    "corw0": _sb(2, "float32"), "corw": _sb(2, "float32"), "quad": _sb(2, "float32"), "tok0": _sb(2, "float32"),
    "tok": _sb(2, "float32"), "k4": _sb(8, "int32"), "plq": _sb(8, "uint16"), "lo": _sb(2, "float32"),
    "hi": _sb(2, "float32"), "pcol": _sb(2, "float32"), "ibias": _sb(2, "float32"), "bl32": _sb(32, "int32"),
    "bl": _sb(32, "uint16"),
    "de": _sb(16, "int32"), "de2": _sb(16, "int32"), "da": _sb(16, "bfloat16"), "db": _sb(16, "bfloat16"),
    "d0": _sb(512, "bfloat16"), "dg": _sb(32, "int32"), "dg2": _sb(32, "int32"), "dga": _sb(32, "bfloat16"),
    "dgb": _sb(32, "bfloat16"), "d4": _sb(32, "bfloat16"), "zz": _sb(136, "bfloat16"),
    "idv0": _sb(128, "bfloat16"), "idv": _sb(128, "bfloat16"),
    "ss": _sb(512, "float32"), "vc": _sb(4, "float32"), "sg": _sb(512, "bfloat16"), "sgb": _sb(768, "bfloat16"),
    "cb": _sb(2080, "bfloat16"), "es": _sb(768, "bfloat16"), "z1": _sb(544, "bfloat16"),
    "sl": _sb(128, "float32"), "so": _sb(512, "float32"), "tr": _sb(512, "float32"), "v16": _sb(16, "float32"),
    "rs": _sb(16, "float32"), "r1": _sb(16, "float32"), "rr": _sb(16, "float32"), "bx": _sb(512, "float32"),
    "sb": _sb(512, "float32"), "v1": _sb(4, "float32"), "sg2": _sb(768, "bfloat16"), "c2": _sb(1600, "bfloat16"),
    "z2": _sb(800, "bfloat16"), "li": _sb(32, "uint16"), "ia": _sb(16, "bfloat16"), "ib": _sb(16, "bfloat16"),
    "inn": _sb(512, "bfloat16"), "iw": _sb(512, "bfloat16"), "q2": _sb(8, "uint16"), "gid": _sb(128, "float32"),
    "ysb": _sb(512, "float32"),
    "ps": ("psum", [128, 4096], "float32"),
}
for _k in ("1", "2"):
    SCRATCH.update({"pt" + _k: _sb(32, "bfloat16"), "pg" + _k: _sb(32, "float16"), "pw" + _k: _sb(8, "uint16"),
                    "wi" + _k: _sb(512, "bfloat16"), "wx" + _k: _sb(512, "float16"), "ge" + _k: _sb(32, "float16"),
                    "gm" + _k: _sb(32, "float16"), "lw" + _k: _sb(32, "uint16")})
SEMAPHORES = ["v", "a", "t", "q", "du", "dx0", "dx1", "dx2", "dx3", "dw", "dst",
              "rem_s", "rem_c", "rem_p", "rem_i", "loc"]


def _routes(core, cores, topo):
    far = [c for c in cores if c != core and topo.chip(c) != topo.chip(core)]
    near = [c for c in cores if c != core and topo.chip(c) == topo.chip(core)]
    out, used = {}, set()
    for i, c in enumerate(far):
        e = topo.engines(core, c)
        k = 1
        while 2 * k * len(far) <= len(e):
            k *= 2
        out[c] = e[i * k:i * k + k]
        used.update(out[c])
    for i, c in enumerate(near):
        e = [n for n in topo.engines(core, c) if n not in used]
        k = 1
        while 2 * k * len(near) <= len(e):
            k *= 2
        out[c] = e[i * k:i * k + k]
    return out


def rank_program(g, core, T, topo):
    rank = T.rank_of(core)
    if rank is None:
        return
    cores = T.cores
    others = [d for d in range(N) if d != rank]
    routes = _routes(core, cores, topo)
    FEW = 4

    def arrive(sem):
        n = [len(_routes(c, cores, topo)[core]) for c in cores if c != core]
        return (sem, sum(min(k, FEW) for k in n) if sem == "rem_s" else sum(n))

    U32, U8 = dt.uint32, dt.uint8

    V = {"q": g.vector, "sem": "v", "n": 0, "seen": {}}
    S = {"q": g.scalar, "sem": "a", "n": 0, "seen": {}}
    P = {"q": g.tensor, "sem": "t", "n": 0, "seen": {}}
    G = {"q": g, "sem": "q", "n": 0, "seen": {}}
    Y = {"q": g.sync, "sem": None, "n": 0, "seen": {}}
    dmas = {}

    def need(E, deps):
        for s, n in deps:
            if E["seen"].get(s, 0) < n:
                E["q"].wait_ge(T.sem[s], n)
                E["seen"][s] = n

    def op(E, deps, call, *a, **k):
        need(E, deps)
        call(*a, **k).then_inc(T.sem[E["sem"]], 1)
        E["n"] += 1
        return (E["sem"], E["n"])

    def dma(E, deps, out, in_, sem):
        need(E, deps)
        E["q"].dma_start(out, in_).then_inc(T.sem[sem], 16)
        dmas[sem] = dmas.get(sem, 0) + 16
        return (sem, dmas[sem])

    def send(deps, pieces, sem):
        need(G, deps)
        tr = []
        for d, src, dst in pieces:
            rid, pid, _ = topo.addr(cores[d])
            engines = routes[cores[d]][:FEW] if sem == "rem_s" else routes[cores[d]]
            tr.append(RemoteDMATransfer(dst_ids=[DstId(rid=rid, pnc=pid)],
                                        dma_engine_mask=sum(1 << e for e in engines),
                                        remote_sem=T.sem[sem], src=src, dst=dst))
            dmas["loc"] = dmas.get("loc", 0) + len(engines)
        g.remote_dma_fused(tr, local_sem=T.sem.loc)

    vec, act, pe = g.vector, g.scalar.activation, g.tensor.matmul_mx
    cp, ts, tt, scan = vec.tensor_copy, vec.tensor_scalar, vec.tensor_tensor, vec.tensor_tensor_scan

    def r(c, w=128):
        return slice(w * c, w * c + w)

    def iota(out, pattern, base, mult, small=True):
        return op(G, [], g.iota, out, pattern, base, mult, allow_small_or_imprecise_dtypes=small)

    dx = [None] * 4
    dx[0] = dma(Y, [], T.xt[:, r(0, 512)], T.x[:, r(0, 512)], "dx0")
    du = dma(S, [], T.ut[:, 0:8], T.u[:, 0:8], "du")
    for c in (1, 2, 3):
        dx[c] = dma(S if c & 1 else Y, [], T.xt[:, r(c, 512)], T.x[:, r(c, 512)], "dx%d" % c)
    dw = dma(Y, [], T.wt[:], T.w[:], "dw")

    k_ip = iota(T.ip[:], [[0, 2]], 0, 1, False)
    k_de = iota(T.de[:], [[1, 16]], 2048, -1, False)
    k_dg = iota(T.dg[:], [[4, 32]], 2051, -1, False)
    k_k4 = iota(T.k4[:], [[4, 8]], 0, 0, False)
    mh = op(V, [], vec.memset, T.half[:], 0.5)
    m0 = op(V, [], vec.memset, T.ut[:, 8:512], 0.0)
    mz = op(V, [], vec.memset, T.zoff[:], 0)
    k_tri = op(G, [mh], g.affine_select, T.tri[:], T.half[:], [[-1, 128]], A.is_gt, -0.5, 0, 1)
    k_i0 = iota(T.idv0[:], [[4, 8], [1, 4], [128, 4]], -256, 0)
    for c in range(4):
        iota(T.cb[:, 520 * c + 512:520 * c + 520], [[0, 8]], 0, 0)
    k_zz = iota(T.zz[:], [[0, 136]], 0, 0)
    mw1 = iota(T.wi1[:], [[0, 512]], -512, 0)
    k_bl = iota(T.bl32[:], [[1, 16], [0, 2]], 0, 0, False)
    for s in range(N):
        for b in (192, 392):
            iota(T.c2[:, 400 * s + b:400 * s + b + 8], [[0, 8]], 0, 0)
    k_pc = iota(T.pcol[:], [[0, 2]], -256, 1)
    mi = iota(T.inn[:], [[1, 4], [0, 128]], 0, 0)
    a96 = op(V, [k_ip], ts, T.p96[:], T.ip[:], 96, None, A.bitwise_and)
    a3 = op(V, [k_ip], ts, T.r3[:], T.ip[:], 3, None, A.bitwise_and)
    a15 = op(V, [k_ip], ts, T.p15[:], T.ip[:], 15, None, A.bitwise_and)
    a12 = op(V, [k_ip], ts, T.p12[:], T.ip[:], 12, None, A.bitwise_and)
    k_qd = op(V, [a96], ts, T.quad[:], T.p96[:], 1, None, A.mult)
    ade = op(V, [k_de], ts, T.de2[:], T.de[:], 15, None, A.bitwise_and)
    adg = op(V, [k_dg], ts, T.dg2[:], T.dg[:], 12, None, A.bitwise_and)
    k_c0 = op(V, [a15], ts, T.corr0[:], T.p15[:], 15, 1024, A.is_lt, A.mult)
    k_w0 = op(V, [a12], ts, T.corw0[:], T.p12[:], 12, 1024, A.is_lt, A.mult)
    for i in range(4):
        ms = op(S, [mh], act, T.so[:, r(i)], T.half[:], F.Copy, 0.0, -1e29)
    k_id = op(S, [k_i0, k_qd], act, T.idv[:], T.idv0[:], F.Identity, T.quad[:, 0:1])

    qu = op(V, [m0, du], vec.quantize_mx, T.uq[:], T.us[:], T.ut[:])
    ub = op(V, [qu, mz], cp, T.ubq[:, 0:128].bitcast(U32), T.uq[:, 0:128].bitcast(U32).indirect(T.zoff[:, 0:8]))
    ubs = op(S, [qu, mz], act, T.ubs[:, 0:128], T.us[:, 0:128].indirect(T.zoff[:, 0:8]), F.Copy)

    qx, pv, psc, vcol, sc, sgn = [None] * 4, [None] * 4, [None] * 4, [None] * 4, [None] * 4, [None] * 4
    sgb = {}

    def quant(c):
        qx[c] = op(V, [dx[c]], vec.quantize_mx, T.xq[:, r(c)], T.xs[:, r(c)], T.xt[:, r(c, 512)])
        b = 512 * (4 + c)
        pv[c] = op(P, [qx[c], qu], pe, T.ps[:, b:b + 128], T.xq[:, r(c)], T.xs[:, r(c)], T.uq[:], T.us[:], True, True)
        b = 512 * c
        psc[c] = op(P, [ub, ubs], pe, T.ps[:, b:b + 128], T.ubq[:], T.ubs[:], T.xq[:, r(c)], T.xs[:, r(c)], True, True)

    def cb(c, a, b):
        return T.cb[:, 520 * c + a:520 * c + b]

    def at_b(c, e):
        return r(c * (c - 1) // 2 + e)

    def work_a(c):
        row = T.ps[:, 512 * c:512 * c + 128]
        vcol[c] = op(V, [pv[c]], cp, T.vc[:, c:c + 1], T.ps[:, 512 * (4 + c):512 * (4 + c) + 1])
        for e in range(c):
            sgb[c, e] = op(S, [psc[c], vcol[e]], act, T.sgb[:, at_b(c, e)], row, F.Sign, T.vc[:, e:e + 1], -1.0)
        sgn[c] = op(S, [psc[c], vcol[c]], act, T.sg[:, r(c)], row, F.Sign, T.vc[:, c:c + 1], -1.0)
        sc[c] = op(S, [], act, T.ss[:, r(c)], row, F.Copy)
        if c:
            return op(V, [vcol[c], sc[c - 1]], ts, cb(c, 0, 128 * c), T.ss[:, 0:128 * c], T.vc[:, c:c + 1], None, A.is_ge)

    def work_b(c, e):
        return op(V, [sgb[c, e]], ts, cb(e, 128 * c, 128 * c + 128), T.sgb[:, at_b(c, e)], 0.0, None, A.is_lt)

    def work_d(c):
        return op(V, [sgn[c], k_tri], tt, cb(c, 128 * c, 128 * c + 128), T.sg[:, r(c)], T.tri[:], A.is_lt)

    def early(c, dep):
        return op(V, [dep], scan, T.es[:, r(c, 192)], cb(c, 0, 192), cb(c, 192, 384), -256.0, A.add, A.add)

    def late(c, dep):
        return op(V, dep + [k_zz], scan, T.z1[:, c:544:4], cb(c, 384, 520), T.zz[:, 0:136],
                  T.es[:, 192 * c + 191:192 * c + 192], A.add, A.add)

    quant(0)
    quant(1)
    k_ga = op(V, [adg], ts, T.dga[:], T.dg2[:], 0, -4096, A.is_equal, A.mult)
    k_gb = op(V, [adg], ts, T.dgb[:], T.dg2[:], 4, 1024, A.is_equal, A.mult)
    k_da = op(V, [ade], ts, T.da[:], T.de2[:], 0, -4096, A.is_equal, A.mult)
    k_db = op(V, [ade], ts, T.db[:], T.de2[:], 1, 1024, A.is_equal, A.mult)
    k_t0 = op(V, [k_qd], ts, T.tok0[:], T.r3[:], 128, T.quad[:, 0:1], A.mult, A.add)
    work_a(0)
    k_d4 = op(V, [k_ga, k_gb], tt, T.d4[:], T.dga[:], T.dgb[:], A.add)
    k_d0 = op(V, [k_da, k_db], tt, T.d0[:, 0:16], T.da[:], T.db[:], A.add)
    k_co = op(V, [k_c0], ts, T.corr[:], T.corr0[:], 256, None, A.subtract)
    k_cw = op(V, [k_w0], ts, T.corw[:], T.corw0[:], 256, None, A.subtract)
    k_tk = op(V, [k_t0], ts, T.tok[:], T.p12[:], 0.25, T.tok0[:, 0:1], A.mult, A.add)
    work_d(0)
    k_pl = op(V, [k_tk, k_k4], ts, T.plq[:], T.k4[:], T.tok[:, 0:1], None, A.add)
    quant(2)
    work_a(1)
    work_b(1, 0)
    work_d(1)
    work_a(2)
    quant(3)
    b0 = work_b(2, 0)
    b1 = work_b(2, 1)
    b2 = work_d(2)
    e0 = early(0, b0)
    e1 = early(1, b1)
    e2 = early(2, b2)
    w3 = work_a(3)
    b0 = work_b(3, 0)
    b1 = work_b(3, 1)
    b2 = work_b(3, 2)
    e3 = early(3, w3)
    b3 = work_d(3)
    late(0, [b0, e0])
    late(1, [b1, e1])
    late(2, [b2, e2])
    fin = late(3, [b3, e3])
    sl = op(S, [k_pl, sc[3]], act, T.sl[:, 0:128], T.ss[:, 0:512].indirect(T.plq[:, 0:8]), F.Copy)
    kd = k_d0
    for n in (16, 32, 64, 128, 256):
        kd = op(S, [kd], act, T.d0[:, n:2 * n], T.d0[:, 0:n], F.Copy)
    for i in range(4):
        mw2 = op(S, [mh], act, T.wi2[:, r(i)], T.half[:], F.Copy, 0.0, -1024.0)

    def offsets(fin, z, k, fill=None):
        x = op(V, [fin], vec.transpose, T["pt" + k][:], z)
        if fill:
            fill()
        x = op(V, [x, k_d4], scan, T["pg" + k][:], T.d4[:], T["pt" + k][:], 0.0, A.add, A.max)
        return op(V, [x, k_cw], ts, T["pw" + k][:, 0:8], T["pg" + k][:, 3:32:4], T.corw[:, 0:1], None, A.subtract)

    def scatter(x, k, mw):
        return op(V, [x, k_id, mw], cp, T["wi" + k][:, 0:512].indirect(T["pw" + k][:, 0:8]), T.idv[:, 0:128])

    def diagonal(x, k):
        return op(V, [x, kd], scan, T["wx" + k][:], T.d0[:], T["wi" + k][:], 0.0, A.add, A.max)

    def quadrants(x, mid, out, w, src):
        for a in range(4):
            p, o = slice(32 * a, 32 * a + 32), slice(32 * (a ^ 1), 32 * (a ^ 1) + 32)
            y = op(V, x, tt, mid[p, 0:w], src(p), src(o), A.max)
        for a in range(2):
            p, o = slice(64 * a, 64 * a + 64), slice(64 * (a ^ 1), 64 * (a ^ 1) + 64)
            z = op(V, [y], tt, out[p, 0:w], mid[p, 0:w], mid[o, 0:w], A.max)
        return z

    def number_list(x, k):
        wx = T["wx" + k]
        x = quadrants([x], T["ge" + k], T["gm" + k], 32, lambda p: wx[p, 15:512:16])
        return x, op(V, [x, k_co], ts, T["lw" + k][:, 0:32], T["gm" + k][:, 0:32], T.corr[:, 0:1], None, A.subtract)

    pw = offsets(fin, T.z1[:, 512:544], "1")
    so = op(V, [pw, sl, ms], cp, T.so[:, 0:512].indirect(T.pw1[:, 0:8]), T.sl[:, 0:128])
    wi = scatter(pw, "1", mw1)
    x = op(V, [so], vec.transpose, T.tr[:], T.so[:])
    wx = diagonal(wi, "1")
    v16 = op(V, [x], cp, T.v16[:], T.tr[:, 0:512:32])
    send([v16], [(d, T.v16[:, 4 * d:4 * d + 4], T.rs[:, 4 * rank:4 * rank + 4]) for d in others], "rem_s")
    rso = op(S, [v16], act, T.rs[:, 4 * rank:4 * rank + 4], T.v16[:, 4 * rank:4 * rank + 4], F.Copy)
    gm, lw = number_list(wx, "1")
    send([lw], [(d, T.lw1[:, 8 * d:8 * d + 8], T.li[:, 8 * rank:8 * rank + 8]) for d in others], "rem_i")

    spans = []
    for i, d in enumerate(others):
        if spans and spans[-1][1] + spans[-1][2] == d:
            spans[-1][2] += 1
        else:
            spans.append([i, d, 1])
    for i, d, n in spans:
        of = T.lw1[:, 8 * d:8 * d + 8 * n]
        at = slice(128 * i, 128 * i + 128 * n)
        pq = op(V, [lw], cp, T.sq[:, at].bitcast(U32), T.xq[:, 0:512].bitcast(U32).indirect(of))
        pp = op(S, [lw], act, T.sp[:, at], T.xs[:, 0:512].indirect(of), F.Copy)
    send([pq], [(d, T.sq[:, r(i)].bitcast(U8), T.lq[:, r(rank)].bitcast(U8)) for i, d in enumerate(others)], "rem_c")
    send([pp], [(d, T.sp[:, r(i)], T.lp[:, r(rank)]) for i, d in enumerate(others)], "rem_p")

    of = T.lw1[:, 8 * rank:8 * rank + 8]
    sbo = op(V, [lw], cp, T.sb[:, r(rank)], T.ss[:, 0:512].indirect(of))
    k_bl = op(V, [k_bl], cp, T.bl[:], T.bl32[:])
    oq = op(V, [lw], cp, T.lq[:, r(rank)].bitcast(U32), T.xq[:, 0:512].bitcast(U32).indirect(of))
    ow = op(S, [lw], act, T.lp[:, r(rank)], T.xs[:, 0:512].indirect(of), F.Copy)
    lio = op(V, [lw], cp, T.li[:, 8 * rank:8 * rank + 8], of)
    a16 = op(V, [k_ip], ts, T.p16[:], T.ip[:], 16, None, A.bitwise_and)
    a31 = op(V, [k_ip], ts, T.p31[:], T.ip[:], 31, None, A.bitwise_and)
    k_lo = op(V, [a16], ts, T.lo[:], T.p16[:], 16, None, A.is_lt)
    k_hi = op(V, [a16], ts, T.hi[:], T.p16[:], 16, None, A.is_equal)
    k_ib = op(V, [a31], ts, T.ibias[:], T.p31[:], 1, 256, A.is_equal, A.mult)
    qw = op(V, [dw], vec.quantize_mx, T.wq[:], T.ws[:], T.wt[:])

    rr = quadrants([arrive("rem_s"), rso], T.r1, T.rr, 16, lambda p: T.rs[p, 0:16])
    sx = others[2]
    bx = {sx: op(S, [rr, k_bl], act, T.bx[:, r(sx)], T.rr[:, 0:16].indirect(T.bl[:, 8 * sx:8 * sx + 8]), F.Copy)}
    for a in range(4):
        v1 = op(S, [rr], act, T.v1[32 * a:32 * a + 32, 0:4], T.rr[32 * a:32 * a + 32, a:16:4], F.Copy)
    for d in others[:2]:
        bx[d] = op(V, [rr, k_bl], cp, T.bx[:, r(d)], T.rr[:, 0:16].indirect(T.bl[:, 8 * d:8 * d + 8]))
    for d in others:
        tb = op(V, [bx[d]], vec.transpose, T.sb[:, r(d)], T.bx[:, r(d)])

    def seg(s):
        return [(0, 128 * s, 0, True)] * (s > 0) + [(128 * s + 128, 512, 128 * s, False)] * (s < 3)

    sg2 = {}
    for s in (2, 3):
        for lo, hi, at, ge in seg(s):
            o = 384 * (s - 2) + at
            sg2[s] = op(S, [v1, tb, sbo], act, T.sg2[:, o:o + hi - lo], T.sb[:, lo:hi], F.Sign, T.v1[:, s:s + 1], -1.0)
    done = []
    for s in range(N):
        for lo, hi, at, ge in seg(s):
            end = at + hi - lo
            for b, e in ([(at, 192), (192, end)] if at < 192 < end else [(at, end)]):
                w = 400 * s + b + 8 * (b >= 192)
                out = T.c2[:, w:w + e - b]
                if s < 2:
                    x = op(V, [v1, tb, sbo], ts, out, T.sb[:, lo + b - at:lo + e - at], T.v1[:, s:s + 1], None,
                           A.is_ge if ge else A.is_gt)
                else:
                    o = 384 * (s - 2)
                    x = op(V, [sg2[s]], ts, out, T.sg2[:, o + b:o + e], 0.0, None, A.is_le if ge else A.is_lt)
        done.append(x)
    for s in range(N):
        fin2 = op(V, [done[s], k_pc], scan, T.z2[:, s:800:4], T.c2[:, 400 * s:400 * s + 200],
                  T.c2[:, 400 * s + 200:400 * s + 400], T.pcol[:, 0:1], A.add, A.add)

    ids = []

    def halves():
        ids.append(op(V, [lio, k_lo, arrive("rem_i")], ts, T.ia[:], T.li[:, 0:32:2], 256, T.lo[:, 0:1], A.subtract, A.mult))
        ids.append(op(V, [k_hi], ts, T.ib[:], T.li[:, 1:32:2], 256, T.hi[:, 0:1], A.subtract, A.mult))

    x = offsets(fin2, T.z2[:, 768:800], "2", halves)
    ic = op(V, ids + [mi], tt, T.inn[:, 1:512:32], T.ia[:], T.ib[:], A.add)
    x = scatter(x, "2", mw2)
    x = diagonal(x, "2")
    iw = op(V, [ic], vec.transpose, T.iw[:], T.inn[:])
    gm, lm = number_list(x, "2")

    def quad_list(a):
        p = slice(32 * a, 32 * a + 32)
        return op(V, [gm], ts, T.q2[p, 0:8], T.gm2[p, 8 * a:8 * a + 8], T.corr[p, 0:1], None, A.subtract)

    quad_list(0)
    quad_list(1)
    ym = [None] * 4
    for k in range(4):
        of = T.lw2[:, 8 * k:8 * k + 8]
        a = op(V, [lm, oq, arrive("rem_c")], cp, T.fq[:, r(k)].bitcast(U32), T.lq[:, 0:512].bitcast(U32).indirect(of))
        b = op(S, [lm, ow, arrive("rem_p")], act, T.fp[:, r(k)], T.lp[:, 0:512].indirect(of), F.Copy)
        ym[k] = op(P, [a, b, qw], pe, T.ps[:, 512 * k:512 * k + 128], T.wq[:, r(k)], T.ws[:, r(k)], T.fq[:, r(k)], T.fp[:, r(k)], True, True)
    quad_list(2)
    ql = quad_list(3)
    for k in range(3):
        yc = op(S, [ym[k]], act, T.ysb[:, r(k)], T.ps[:, 512 * k:512 * k + 128], F.Copy)
        dma(Y, [yc], T.y[:, r(k)], T.ysb[:, r(k)], "dst")
    ig = op(V, [ql, iw, k_ib], ts, T.gid[:, 0:128], T.iw[:, 0:512].indirect(T.q2[:, 0:8]), T.ibias[:, 0:1], None, A.add)
    for a in range(4):
        dma(Y, [ig], T.ids[:, r(a)], T.gid[32 * a:32 * a + 2, 0:128], "dst")
    yc = op(V, [ym[3]], cp, T.ysb[:, r(3)], T.ps[:, 512 * 3:512 * 3 + 128])
    dma(S, [yc], T.y[:, r(3)], T.ysb[:, r(3)], "dst")

    need(Y, [("dst", dmas["dst"])])
    need(G, [("loc", dmas["loc"]), ("v", V["n"]), ("a", S["n"]), ("t", P["n"]), ("q", G["n"])])
